import numpy as np
import ml_dtypes

BF16 = ml_dtypes.bfloat16


def bf(x):
    return np.asarray(x, np.float32).astype(BF16)


def f32(x):
    return np.asarray(x, np.float32)


def f64(x):
    return np.asarray(x).astype(np.float64)


def striped(idx):
    return np.tile(idx.reshape(-1, 16).T, (8, 1))


def rows(idx, k):
    return np.tile(idx, (k, 1))


def look(tab, idx):
    return np.take_along_axis(f64(tab), rows(idx, len(tab)), axis=1)


K, S, V, N, M = 256, 2048, 1024, 1024, 512


def setup_inputs():
    return {"tab": f32(np.random.standard_normal((2, K, S))), "w": bf(np.random.standard_normal((K, M)) / np.sqrt(K)), "b": f32(0.5 * np.random.standard_normal((M, 1))), "offs": striped(np.random.permutation(S)[:N])}


def reference(tab, w, b, offs):
    idx = offs[:16].T.reshape(-1)
    x = (np.minimum(np.maximum(look(tab[0], idx), -1.25), 1.0)) * (np.tanh(look(tab[1], idx)))
    return np.maximum(f64(w).T @ x + f64(b), 0.0)

@@ -1,0 +1,77 @@
+import concourse.mybir as mybir
+
+F32, BF16, U16 = mybir.dt.float32, mybir.dt.bfloat16, mybir.dt.uint16
+MAX, MIN, MULT, ADD = (
+    mybir.AluOpType.max,
+    mybir.AluOpType.min,
+    mybir.AluOpType.mult,
+    mybir.AluOpType.add,
+)
+TANH, RELU = mybir.ActivationFunctionType.Tanh, mybir.ActivationFunctionType.Relu
+
+P = 128
+K, S, N, M = 256, 2048, 1024, 512
+KB = K // P
+MB = M // P
+PIECE = 512
+PIECES = N // PIECE
+
+FLOPS = 2 * K * M * N
+
+
+def tile_lookup_vg_cliptanh_relu_kernel(tc, tab, w, b, offs, out):
+    nc = tc.nc
+    with (
+        tc.tile_pool(name="held", bufs=1) as held,
+        tc.tile_pool(name="work", bufs=1) as work,
+        tc.psum_pool(name="psum", bufs=1) as psum,
+    ):
+        offsets = held.tile([P, N // 16], U16, name="offsets")
+        nc.sync.dma_start(offsets[:], offs)
+
+        values = [held.tile([P, S], F32, name=f"values{k}") for k in range(KB)]
+        gates = [held.tile([P, S], F32, name=f"gates{k}") for k in range(KB)]
+        weights = held.tile([P, KB, M], BF16, name="weights")
+        bias = held.tile([P, MB], F32, name="bias")
+
+        nc.sync.dma_start(values[0][:], tab[0, 0:P, :])
+        nc.sync.dma_start(gates[0][:], tab[1, 0:P, :])
+        nc.sync.dma_start(weights[:], w.rearrange("(k p) m -> p k m", p=P))
+        nc.sync.dma_start(bias[:], b.rearrange("(p q) one -> p (q one)", q=MB))
+        nc.sync.dma_start(values[1][:], tab[0, P:K, :])
+        nc.sync.dma_start(gates[1][:], tab[1, P:K, :])
+
+        banks = [
+            [psum.tile([P, PIECE], F32, name=f"bank{c}_{q}") for q in range(MB)]
+            for c in range(PIECES)
+        ]
+        out_rows = out.rearrange("(p q) n -> p q n", q=MB)
+
+        for k in range(KB):
+            for c in range(PIECES):
+                entries = offsets[:, c * PIECE // 16 : (c + 1) * PIECE // 16]
+                clamped = work.tile([P, PIECE], F32, name=f"clamped{k}_{c}")
+                nc.vector.tensor_scalar(
+                    clamped[:], values[k][:].indirect(entries), -1.25, 1.0, MAX, MIN
+                )
+                gate = work.tile([P, PIECE], F32, name=f"gate{k}_{c}")
+                nc.scalar.activation(gate[:], gates[k][:].indirect(entries), TANH)
+                x = work.tile([P, PIECE], BF16, name=f"x{k}_{c}")
+                nc.vector.tensor_tensor(x[:], clamped[:], gate[:], MULT)
+                for q in range(MB):
+                    nc.tensor.matmul(
+                        banks[c][q][:],
+                        weights[:, k, q::MB],
+                        x[:],
+                        start=(k == 0),
+                        stop=(k == KB - 1),
+                    )
+
+        for c in range(PIECES):
+            for q in range(MB):
+                y = work.tile([P, PIECE], F32, name=f"y{c}_{q}")
+                if q % 2 == 0:
+                    nc.scalar.activation(y[:], banks[c][q][:], RELU, bias=bias[:, q : q + 1])
+                else:
+                    nc.vector.tensor_scalar(y[:], banks[c][q][:], bias[:, q : q + 1], 0.0, ADD, MAX)
+                nc.sync.dma_start(out_rows[:, q, c * PIECE : (c + 1) * PIECE], y[:])

@@ -13,7 +13,7 @@ P = 128
 K, S, N, M = 256, 2048, 1024, 512
 KB = K // P
 MB = M // P
-PIECE = 512
+PIECE = 256
 PIECES = N // PIECE
 
 FLOPS = 2 * K * M * N
@@ -24,54 +24,57 @@ def tile_lookup_vg_cliptanh_relu_kernel(tc, tab, w, b, offs, out):
     with (
         tc.tile_pool(name="held", bufs=1) as held,
         tc.tile_pool(name="work", bufs=1) as work,
-        tc.psum_pool(name="psum", bufs=1) as psum,
+        tc.psum_pool(name="psum", bufs=2) as psum,
     ):
         offsets = held.tile([P, N // 16], U16, name="offsets")
         nc.sync.dma_start(offsets[:], offs)
 
         values = [held.tile([P, S], F32, name=f"values{k}") for k in range(KB)]
         gates = [held.tile([P, S], F32, name=f"gates{k}") for k in range(KB)]
-        weights = held.tile([P, KB, M], BF16, name="weights")
+        weights = [held.tile([P, M], BF16, name=f"weights{k}") for k in range(KB)]
         bias = held.tile([P, MB], F32, name="bias")
 
         nc.sync.dma_start(values[0][:], tab[0, 0:P, :])
         nc.sync.dma_start(gates[0][:], tab[1, 0:P, :])
-        nc.sync.dma_start(weights[:], w.rearrange("(k p) m -> p k m", p=P))
+        nc.sync.dma_start(weights[0][:], w[0:P, :])
         nc.sync.dma_start(bias[:], b.rearrange("(p q) one -> p (q one)", q=MB))
         nc.sync.dma_start(values[1][:], tab[0, P:K, :])
         nc.sync.dma_start(gates[1][:], tab[1, P:K, :])
+        nc.sync.dma_start(weights[1][:], w[P:K, :])
 
-        banks = [
-            [psum.tile([P, PIECE], F32, name=f"bank{c}_{q}") for q in range(MB)]
-            for c in range(PIECES)
-        ]
         out_rows = out.rearrange("(p q) n -> p q n", q=MB)
 
-        for k in range(KB):
-            for c in range(PIECES):
-                entries = offsets[:, c * PIECE // 16 : (c + 1) * PIECE // 16]
-                clamped = work.tile([P, PIECE], F32, name=f"clamped{k}_{c}")
-                nc.vector.tensor_scalar(
-                    clamped[:], values[k][:].indirect(entries), -1.25, 1.0, MAX, MIN
-                )
-                gate = work.tile([P, PIECE], F32, name=f"gate{k}_{c}")
-                nc.scalar.activation(gate[:], gates[k][:].indirect(entries), TANH)
-                x = work.tile([P, PIECE], BF16, name=f"x{k}_{c}")
-                nc.vector.tensor_tensor(x[:], clamped[:], gate[:], MULT)
+        def look_up(k, c):
+            entries = offsets[:, c * PIECE // 16 : (c + 1) * PIECE // 16]
+            clamped = work.tile([P, PIECE], F32, name=f"clamped{k}_{c}")
+            nc.vector.tensor_scalar(clamped[:], values[k][:].indirect(entries), -1.25, 1.0, MAX, MIN)
+            gate = work.tile([P, PIECE], F32, name=f"gate{k}_{c}")
+            nc.scalar.activation(gate[:], gates[k][:].indirect(entries), TANH)
+            x = work.tile([P, PIECE], BF16, name=f"x{k}_{c}")
+            nc.vector.tensor_tensor(x[:], clamped[:], gate[:], MULT)
+            return x
+
+        x_first = [look_up(0, c) for c in range(PIECES)]
+        for c in range(PIECES):
+            x_pair = (x_first[c], look_up(1, c))
+            banks = [psum.tile([P, PIECE], F32, name=f"bank{q}") for q in range(MB)]
+            for k in range(KB):
                 for q in range(MB):
                     nc.tensor.matmul(
-                        banks[c][q][:],
-                        weights[:, k, q::MB],
-                        x[:],
+                        banks[q][:],
+                        weights[k][:, q::MB],
+                        x_pair[k][:],
                         start=(k == 0),
                         stop=(k == KB - 1),
                     )
-
-        for c in range(PIECES):
-            for q in range(MB):
-                y = work.tile([P, PIECE], F32, name=f"y{c}_{q}")
-                if q % 2 == 0:
-                    nc.scalar.activation(y[:], banks[c][q][:], RELU, bias=bias[:, q : q + 1])
-                else:
-                    nc.vector.tensor_scalar(y[:], banks[c][q][:], bias[:, q : q + 1], 0.0, ADD, MAX)
-                nc.sync.dma_start(out_rows[:, q, c * PIECE : (c + 1) * PIECE], y[:])
+            for h in range(MB // 2):
+                y = work.tile([P, 2, PIECE], F32, name=f"y{c}_{h}")
+                for i in range(2):
+                    q = 2 * h + i
+                    if i == 0:
+                        nc.scalar.activation(y[:, i, :], banks[q][:], RELU, bias=bias[:, q : q + 1])
+                    else:
+                        nc.vector.tensor_scalar(y[:, i, :], banks[q][:], bias[:, q : q + 1], 0.0, ADD, MAX)
+                nc.sync.dma_start(
+                    out_rows[:, 2 * h : 2 * h + 2, c * PIECE : (c + 1) * PIECE], y[:]
+                )

@@ -34,12 +34,17 @@ def tile_lookup_vg_cliptanh_relu_kernel(tc, tab, w, b, offs, out):
         weights = [held.tile([P, M], BF16, name=f"weights{k}") for k in range(KB)]
         bias = held.tile([P, MB], F32, name="bias")
 
+        zero = held.tile([P, 1], F32, name="zero")
+        nc.gpsimd.memset(zero[:], 0.0)
+        warm = held.tile([P, 1], F32, name="warm")
+        nc.scalar.activation(warm[:], zero[:], TANH)
+
         nc.sync.dma_start(values[0][:], tab[0, 0:P, :])
         nc.sync.dma_start(gates[0][:], tab[1, 0:P, :])
-        nc.sync.dma_start(weights[0][:], w[0:P, :])
-        nc.sync.dma_start(bias[:], b.rearrange("(p q) one -> p (q one)", q=MB))
-        nc.sync.dma_start(values[1][:], tab[0, P:K, :])
         nc.sync.dma_start(gates[1][:], tab[1, P:K, :])
+        nc.sync.dma_start(bias[:], b.rearrange("(p q) one -> p (q one)", q=MB))
+        nc.sync.dma_start(weights[0][:], w[0:P, :])
+        nc.sync.dma_start(values[1][:], tab[0, P:K, :])
         nc.sync.dma_start(weights[1][:], w[P:K, :])
 
         out_rows = out.rearrange("(p q) n -> p q n", q=MB)
@@ -71,7 +76,7 @@ def tile_lookup_vg_cliptanh_relu_kernel(tc, tab, w, b, offs, out):
                 y = work.tile([P, 2, PIECE], F32, name=f"y{c}_{h}")
                 for i in range(2):
                     q = 2 * h + i
-                    if i == 0:
+                    if c < PIECES // 2 or i == 0:
                         nc.scalar.activation(y[:, i, :], banks[q][:], RELU, bias=bias[:, q : q + 1])
                     else:
                         nc.vector.tensor_scalar(y[:, i, :], banks[q][:], bias[:, q : q + 1], 0.0, ADD, MAX)

@@ -13,8 +13,8 @@ P = 128
 K, S, N, M = 256, 2048, 1024, 512
 KB = K // P
 MB = M // P
-PIECE = 256
-PIECES = N // PIECE
+PIECES = (slice(0, N // 4), slice(N // 4, 3 * N // 4), slice(3 * N // 4, N))
+BANK = 512
 
 FLOPS = 2 * K * M * N
 
@@ -50,36 +50,35 @@ def tile_lookup_vg_cliptanh_relu_kernel(tc, tab, w, b, offs, out):
         out_rows = out.rearrange("(p q) n -> p q n", q=MB)
 
         def look_up(k, c):
-            entries = offsets[:, c * PIECE // 16 : (c + 1) * PIECE // 16]
-            clamped = work.tile([P, PIECE], F32, name=f"clamped{k}_{c}")
+            piece = PIECES[c]
+            width = piece.stop - piece.start
+            entries = offsets[:, piece.start // 16 : piece.stop // 16]
+            clamped = work.tile([P, width], F32, name=f"clamped{k}_{c}")
             nc.vector.tensor_scalar(clamped[:], values[k][:].indirect(entries), -1.25, 1.0, MAX, MIN)
-            gate = work.tile([P, PIECE], F32, name=f"gate{k}_{c}")
+            gate = work.tile([P, width], F32, name=f"gate{k}_{c}")
             nc.scalar.activation(gate[:], gates[k][:].indirect(entries), TANH)
-            x = work.tile([P, PIECE], BF16, name=f"x{k}_{c}")
+            x = work.tile([P, width], BF16, name=f"x{k}_{c}")
             nc.vector.tensor_tensor(x[:], clamped[:], gate[:], MULT)
             return x
 
-        x_first = [look_up(0, c) for c in range(PIECES)]
-        for c in range(PIECES):
+        x_first = [look_up(0, c) for c in range(len(PIECES))]
+        for c, piece in enumerate(PIECES):
+            width = piece.stop - piece.start
             x_pair = (x_first[c], look_up(1, c))
-            banks = [psum.tile([P, PIECE], F32, name=f"bank{q}") for q in range(MB)]
+            banks = [psum.tile([P, BANK], F32, name=f"bank{q}") for q in range(MB)]
             for k in range(KB):
                 for q in range(MB):
                     nc.tensor.matmul(
-                        banks[q][:],
+                        banks[q][:, :width],
                         weights[k][:, q::MB],
                         x_pair[k][:],
                         start=(k == 0),
                         stop=(k == KB - 1),
                     )
-            for h in range(MB // 2):
-                y = work.tile([P, 2, PIECE], F32, name=f"y{c}_{h}")
-                for i in range(2):
-                    q = 2 * h + i
-                    if c < PIECES // 2 or i == 0:
-                        nc.scalar.activation(y[:, i, :], banks[q][:], RELU, bias=bias[:, q : q + 1])
-                    else:
-                        nc.vector.tensor_scalar(y[:, i, :], banks[q][:], bias[:, q : q + 1], 0.0, ADD, MAX)
-                nc.sync.dma_start(
-                    out_rows[:, 2 * h : 2 * h + 2, c * PIECE : (c + 1) * PIECE], y[:]
-                )
+            for q in range(MB):
+                y = work.tile([P, width], F32, name=f"y{c}_{q}")
+                if c == 0 or q % 2 == 0:
+                    nc.scalar.activation(y[:], banks[q][:, :width], RELU, bias=bias[:, q : q + 1])
+                else:
+                    nc.vector.tensor_scalar(y[:], banks[q][:, :width], bias[:, q : q + 1], 0.0, ADD, MAX)
+                nc.sync.dma_start(out_rows[:, q, piece], y[:])

import concourse.mybir as mybir

F32, BF16, U16 = mybir.dt.float32, mybir.dt.bfloat16, mybir.dt.uint16
MAX, MIN, MULT, ADD = (
    mybir.AluOpType.max,
    mybir.AluOpType.min,
    mybir.AluOpType.mult,
    mybir.AluOpType.add,
)
TANH, RELU = mybir.ActivationFunctionType.Tanh, mybir.ActivationFunctionType.Relu

P = 128
K, S, N, M = 256, 2048, 1024, 512
KB = K // P
MB = M // P
PIECES = (slice(0, N // 4), slice(N // 4, 3 * N // 4), slice(3 * N // 4, N))
BANK = 512

FLOPS = 2 * K * M * N


def tile_lookup_vg_cliptanh_relu_kernel(tc, tab, w, b, offs, out):
    nc = tc.nc
    with (
        tc.tile_pool(name="held", bufs=1) as held,
        tc.tile_pool(name="work", bufs=1) as work,
        tc.psum_pool(name="psum", bufs=2) as psum,
    ):
        offsets = held.tile([P, N // 16], U16, name="offsets")
        nc.sync.dma_start(offsets[:], offs)

        values = [held.tile([P, S], F32, name=f"values{k}") for k in range(KB)]
        gates = [held.tile([P, S], F32, name=f"gates{k}") for k in range(KB)]
        weights = [held.tile([P, M], BF16, name=f"weights{k}") for k in range(KB)]
        bias = held.tile([P, MB], F32, name="bias")

        zero = held.tile([P, 1], F32, name="zero")
        nc.gpsimd.memset(zero[:], 0.0)
        warm = held.tile([P, 1], F32, name="warm")
        nc.scalar.activation(warm[:], zero[:], TANH)

        nc.sync.dma_start(values[0][:], tab[0, 0:P, :])
        nc.sync.dma_start(gates[0][:], tab[1, 0:P, :])
        nc.sync.dma_start(gates[1][:], tab[1, P:K, :])
        nc.sync.dma_start(bias[:], b.rearrange("(p q) one -> p (q one)", q=MB))
        nc.sync.dma_start(weights[0][:], w[0:P, :])
        nc.sync.dma_start(values[1][:], tab[0, P:K, :])
        nc.sync.dma_start(weights[1][:], w[P:K, :])

        out_rows = out.rearrange("(p q) n -> p q n", q=MB)

        def look_up(k, c):
            piece = PIECES[c]
            width = piece.stop - piece.start
            entries = offsets[:, piece.start // 16 : piece.stop // 16]
            clamped = work.tile([P, width], F32, name=f"clamped{k}_{c}")
            nc.vector.tensor_scalar(clamped[:], values[k][:].indirect(entries), -1.25, 1.0, MAX, MIN)
            gate = work.tile([P, width], F32, name=f"gate{k}_{c}")
            nc.scalar.activation(gate[:], gates[k][:].indirect(entries), TANH)
            x = work.tile([P, width], BF16, name=f"x{k}_{c}")
            nc.vector.tensor_tensor(x[:], clamped[:], gate[:], MULT)
            return x

        x_first = [look_up(0, c) for c in range(len(PIECES))]
        for c, piece in enumerate(PIECES):
            width = piece.stop - piece.start
            x_pair = (x_first[c], look_up(1, c))
            banks = [psum.tile([P, BANK], F32, name=f"bank{q}") for q in range(MB)]
            for k in range(KB):
                for q in range(MB):
                    nc.tensor.matmul(
                        banks[q][:, :width],
                        weights[k][:, q::MB],
                        x_pair[k][:],
                        start=(k == 0),
                        stop=(k == KB - 1),
                    )
            for q in range(MB):
                y = work.tile([P, width], F32, name=f"y{c}_{q}")
                if c == 0 or q % 2 == 0:
                    nc.scalar.activation(y[:], banks[q][:, :width], RELU, bias=bias[:, q : q + 1])
                else:
                    nc.vector.tensor_scalar(y[:], banks[q][:, :width], bias[:, q : q + 1], 0.0, ADD, MAX)
                nc.sync.dma_start(out_rows[:, q, piece], y[:])
